import numpy as np
import ml_dtypes


def mxq(x, axis, fmt="e4m3"):
    dtype, down = {"e4m3": (ml_dtypes.float8_e4m3fn, 7), "e5m2": (ml_dtypes.float8_e5m2, 14)}[fmt]
    v = np.moveaxis(np.asarray(x, np.float32).astype(ml_dtypes.bfloat16).astype(np.float64), axis, -1)
    blocks = v.reshape(v.shape[:-1] + (-1, 32))
    amax = np.abs(blocks).max(-1, keepdims=True)
    byte = np.maximum(np.where(amax > 0, np.frexp(amax)[1] - 1 + 127, 0) - down, 1)
    scale = np.exp2(byte - 127.0)
    codes = (blocks / scale).astype(np.float32).astype(dtype).astype(np.float64)
    return np.moveaxis((codes * scale).reshape(v.shape), -1, axis)


WIDE = False


def mx_kscale(k):
    if not WIDE:
        return np.ones(k)
    levels = np.array([10, -10, 5, -5, 0])
    if k % 512:
        return np.exp2(np.random.permutation(np.resize(levels, k // 32))).repeat(32)
    a = np.empty((k // 512, 16))
    for p in range(k // 512):
        a[p, :8] = np.random.permutation(np.resize(levels, 8))
        for g in range(8):
            far = levels[np.abs(levels - a[p, g]) >= 10]
            a[p, g + 8] = far[np.random.randint(len(far))]
    return np.exp2(a.ravel()).repeat(32)


def f64(x):
    return np.asarray(x).astype(np.float64)


def striped(idx):
    return np.tile(idx.reshape(-1, 16).T, (8, 1)).astype(np.uint16)


def unstriped(offs):
    return offs[:16].T.reshape(-1).astype(np.int64)


def pack_weight(w):
    k, n = w.shape
    w = f64(np.asarray(w, np.float32).astype(ml_dtypes.bfloat16)).reshape(k // 32, 32, n)
    amax = np.abs(w).max(1)
    byte = np.clip(np.where(amax > 0, np.frexp(amax)[1] - 1 + 127 - 7, 1), 1, 254)
    scaled = (w * np.exp2(127.0 - byte)[:, None, :]).reshape(k, n).astype(np.float32)
    words = np.ascontiguousarray(scaled.reshape(k // 512, 128, 4, n).transpose(0, 1, 3, 2)).astype(ml_dtypes.float8_e4m3fn).view(np.uint8)
    return words, np.ascontiguousarray(byte.astype(np.uint8).reshape(k // 512, 16, n))


def unpack_weight(words, scales):
    g, p, n, _ = words.shape
    vals = np.ascontiguousarray(words).view(ml_dtypes.float8_e4m3fn).astype(np.float64) * np.repeat(np.exp2(scales.astype(np.float64) - 127.0), 8, axis=1)[..., None]
    return vals.transpose(0, 1, 3, 2).reshape(g * 512, n)


K, T, S, V, D, N = 1024, 2048, 1024, 256, 3, 256
P = 2 ** 7


def setup_inputs():
    n = np.random.standard_normal
    s = mx_kscale(K)[:, None]
    packed_xT = pack_weight(n((K, T)) * s)
    return {
        "x_words": packed_xT[0],
        "x_scales": packed_xT[1],
        "w0": (n((K, N)) / np.sqrt(K) / s).astype(np.float32),
        "w1": (n((K, N)) / np.sqrt(K) / s).astype(np.float32),
        "w2": (n((K, N)) / np.sqrt(K) / s).astype(np.float32),
        "w3": (n((K, N)) / np.sqrt(K) / s).astype(np.float32),
        "gate": (np.tile(np.random.uniform(0.2, 1.0, (D, 1, V)), (1, P, 1))).astype(np.float32),
        "offs": striped(np.random.permutation(T)[:S]),
    }


def reference(x_words, x_scales, w0, w1, w2, w3, gate, offs):
    xq = unpack_weight(x_words, x_scales)[:, unstriped(offs)]
    y0 = mxq(f64(w0), 0, "e4m3").T @ xq[:, :V]
    y1 = mxq(f64(w1), 0, "e4m3").T @ xq[:, V:2 * V]
    y2 = mxq(f64(w2), 0, "e4m3").T @ xq[:, 2 * V:3 * V]
    y3 = mxq(f64(w3), 0, "e4m3").T @ xq[:, 3 * V:4 * V]
    return np.tanh(y0 + y1 * f64(gate)[0, :1] + y2 * f64(gate)[1, :1] + y3 * f64(gate)[2, :1])

@@ -1,0 +1,184 @@
+from contextlib import ExitStack
+
+import concourse.mybir as mybir
+from concourse.masks import make_identity
+
+K, T, S, V, D, M = 1024, 2048, 1024, 256, 3, 256
+FLOPS = 2 * K * M * S
+
+F32 = mybir.dt.float32
+BF16 = mybir.dt.bfloat16
+I32 = mybir.dt.int32
+U32 = mybir.dt.uint32
+U16 = mybir.dt.uint16
+U8 = mybir.dt.uint8
+FP8X4 = mybir.dt.float8_e4m3fn_x4
+COPY = mybir.ActivationFunctionType.Copy
+TANH = mybir.ActivationFunctionType.Tanh
+MULT = mybir.AluOpType.mult
+ADD = mybir.AluOpType.add
+
+P = 128
+PACK = 4
+K_PASS = P * PACK
+PASSES = K // K_PASS
+HALVES = 2
+LIST_COLS = V // 16
+VECTOR_COLS = 176
+HEAD = 384
+
+
+def tile_picked_zrgcn_tanh_p_kernel(tc, x_words, x_scales, w0, w1, w2, w3, gate, offs, out):
+    nc = tc.nc
+    weights = [w0, w1, w2, w3]
+    parts = [1, 2, 3, 0]
+
+    with ExitStack() as ctx:
+        keep = ctx.enter_context(tc.tile_pool(name="keep", bufs=1))
+        psum = ctx.enter_context(tc.psum_pool(name="psum", bufs=1))
+        psum2 = ctx.enter_context(tc.psum_pool(name="psum2", bufs=2))
+
+        offsets = keep.tile([P, S // 16], U16, name="offsets")
+        scale_table = keep.tile([P, T], U8, name="scale_table", align_bytes=64)
+        gate_rows = keep.tile([P, D, P], F32, name="gate_rows")
+        ident = keep.tile([P, P], F32, name="ident")
+        nc.vector.memset(scale_table[:].bitcast(I32), 0)
+        make_identity(nc, ident[:])
+        nc.gpsimd.memset(gate_rows[:], 0.0)
+
+        raw = {}
+
+        def load_weight(d, o):
+            raw[d, o] = keep.tile([P, PACK, M], F32, name="raw%d%d" % (d, o), align_bytes=64)
+            rows = weights[d][o * K_PASS : (o + 1) * K_PASS, :]
+            nc.sync.dma_start(out=raw[d, o][:], in_=rows.rearrange("(p j) m -> p j m", j=PACK))
+
+        word_table = [keep.tile([P, T], I32, name="word_table%d" % o, align_bytes=64) for o in range(PASSES)]
+        words = [x_words[o].rearrange("p n t -> p (n t)").bitcast(I32) for o in range(PASSES)]
+        nc.sync.dma_start(offsets[:], offs)
+        nc.sync.dma_start(out=word_table[0][:, 0:HEAD], in_=words[0][:, 0:HEAD])
+        for q in range(4):
+            nc.sync.dma_start(
+                out=scale_table[32 * q : 32 * q + 8, :].bitcast(I32),
+                in_=x_scales[:, 4 * q : 4 * q + 4, :].bitcast(I32),
+            )
+        nc.sync.dma_start(out=word_table[0][:, HEAD:T], in_=words[0][:, HEAD:T])
+        nc.sync.dma_start(out=word_table[1][:], in_=words[1])
+        nc.sync.dma_start(out=gate_rows[0:HALVES, :, :], in_=gate[:, 0, :].rearrange("d (h c) -> h d c", h=HALVES))
+        for d in parts:
+            for o in range(PASSES):
+                if (d, o) not in raw:
+                    load_weight(d, o)
+
+        gate_ps = psum.tile([P, D, P], F32, name="gate_ps", tag="self1")
+        for d in range(D):
+            nc.tensor.transpose(gate_ps[:, d, :], gate_rows[:, d, :], ident[:])
+        gate_cols = keep.tile([P, D, HALVES], F32, name="gate_cols")
+        nc.scalar.activation(gate_cols[:], gate_ps[:, :, 0:HALVES], COPY)
+
+        x_sc = keep.tile([P, S], U8, name="x_sc", align_bytes=64)
+        nc.vector.tensor_copy(x_sc[:], scale_table[:].indirect(offsets[:]))
+
+        w_codes, w_sc, grouped = {}, {}, {}
+
+        def cast(d, o, engine, c0, c1):
+            dst = grouped[d, o][:, c0:c1, :].rearrange("p (c i) t -> p c t i", i=4)
+            src = raw[d, o][:, :, c0:c1].rearrange("p t (c i) -> p c t i", i=4)
+            if engine == "vector":
+                nc.vector.tensor_copy(out=dst, in_=src)
+            else:
+                nc.scalar.activation(dst, src, COPY)
+
+        def quantise(d, o, c0, c1):
+            nc.vector.quantize_mx(
+                out=w_codes[d, o][:, c0:c1].bitcast(FP8X4),
+                scales=w_sc[d, o][:, c0:c1],
+                in_=grouped[d, o][:, c0:c1, :].rearrange("p c t -> p (c t)"),
+            )
+
+        def prepare(d, o, plan, cuts):
+            grouped[d, o] = keep.tile([P, M, PACK], BF16, name="grouped%d%d" % (d, o), align_bytes=64)
+            w_codes[d, o] = keep.tile([P, M], U32, name="w_codes%d%d" % (d, o), align_bytes=64)
+            w_sc[d, o] = keep.tile([P, M], U8, name="w_sc%d%d" % (d, o), align_bytes=64)
+            for engine, c0, c1 in plan:
+                cast(d, o, engine, c0, c1)
+            for c0, c1 in cuts:
+                quantise(d, o, c0, c1)
+
+        whole_scalar = [("scalar", 0, M)]
+        shared = [("vector", 0, P), ("scalar", P, M)]
+        last = [("vector", 0, P), ("vector", P, VECTOR_COLS), ("scalar", VECTOR_COLS, M)]
+
+        x0 = keep.tile([P, S], U32, name="x_codes0", align_bytes=64)
+        nc.vector.tensor_copy(x0[:], word_table[0][:].bitcast(U32).indirect(offsets[:]))
+        x_codes = {}
+        for d in parts:
+            x_codes[d, 0] = x0[:, d * V : (d + 1) * V]
+            x1 = keep.tile([P, V], U32, name="x_codes1_%d" % d, align_bytes=64)
+            nc.vector.tensor_copy(
+                x1[:], word_table[1][:].bitcast(U32).indirect(offsets[:, d * LIST_COLS : (d + 1) * LIST_COLS])
+            )
+            x_codes[d, 1] = x1[:]
+
+        prepare(1, 0, whole_scalar, [(0, M)])
+
+        def x_plane(d, o, c0, c1):
+            return x_sc[4 * o : P, d * V + c0 : d * V + c1]
+
+        gated = [psum.tile([P, V], F32, name="gated%d" % mt) for mt in range(HALVES)]
+        for d in (1, 2, 3):
+            y = [psum2.tile([P, M], F32, name="y%d%d" % (d, h), tag="y%d" % h) for h in range(HALVES)]
+            for o in range(PASSES):
+                if (d, o) != (1, 0):
+                    prepare(d, o, whole_scalar if d == 1 else shared, [(0, M)])
+                for h in range(HALVES):
+                    nc.tensor.matmul_mx(
+                        out=y[h][:],
+                        lhsT=x_codes[d, o][:, h * P : (h + 1) * P].bitcast(FP8X4),
+                        lhsT_scale=x_plane(d, o, h * P, (h + 1) * P),
+                        rhs=w_codes[d, o][:].bitcast(FP8X4),
+                        rhs_scale=w_sc[d, o][:],
+                        start=(o == 0),
+                        stop=(o == PASSES - 1),
+                    )
+            for h in range(HALVES):
+                u = keep.tile([P, M], F32, name="u%d%d" % (d, h))
+                g = gate_cols[:, d - 1, h : h + 1]
+                nc.scalar.activation(u[:], y[h][:], COPY, scale=g)
+                for mt in range(HALVES):
+                    nc.tensor.matmul(
+                        gated[mt][:, h * P : (h + 1) * P],
+                        u[:, mt * P : (mt + 1) * P],
+                        ident[:],
+                        is_transpose=True,
+                        start=(d == 1 and h == 0),
+                        stop=(d == D and h == HALVES - 1),
+                    )
+
+        y0 = [psum.tile([P, V], F32, name="y0_%d" % mt, tag="self%d" % mt) for mt in range(HALVES)]
+        for o in range(PASSES):
+            if o == 0:
+                prepare(0, o, shared, [(0, M)])
+            else:
+                prepare(0, o, last, [(0, P), (P, M)])
+            for mt in range(HALVES):
+                nc.tensor.matmul_mx(
+                    out=y0[mt][:],
+                    lhsT=w_codes[0, o][:, mt * P : (mt + 1) * P].bitcast(FP8X4),
+                    lhsT_scale=w_sc[0, o][:, mt * P : (mt + 1) * P],
+                    rhs=x_codes[0, o].bitcast(FP8X4),
+                    rhs_scale=x_plane(0, o, 0, V),
+                    start=(o == 0),
+                    stop=(o == PASSES - 1),
+                )
+        sums = []
+        for mt in range(HALVES):
+            part = keep.tile([P, V], F32, name="part%d" % mt)
+            nc.scalar.activation(part[:], gated[mt][:], COPY)
+            sums.append(part)
+        for mt in range(HALVES):
+            z = keep.tile([P, V], F32, name="z%d" % mt)
+            nc.vector.tensor_tensor(z[:], y0[mt][:], sums[mt][:], ADD)
+            res = keep.tile([P, V], F32, name="res%d" % mt)
+            nc.scalar.activation(res[:], z[:], TANH)
+            nc.sync.dma_start(out=out[mt * P : (mt + 1) * P, :], in_=res[:])

@@ -106,8 +106,8 @@ def tile_picked_zrgcn_tanh_p_kernel(tc, x_words, x_scales, w0, w1, w2, w3, gate,
                 quantise(d, o, c0, c1)
 
         whole_scalar = [("scalar", 0, M)]
-        shared = [("vector", 0, P), ("scalar", P, M)]
-        last = [("vector", 0, P), ("vector", P, VECTOR_COLS), ("scalar", VECTOR_COLS, M)]
+        shared = [("vector", 0, 192), ("scalar", 192, M)]
+        last = [("vector", 0, P), ("vector", P, M)]
 
         x0 = keep.tile([P, S], U32, name="x_codes0", align_bytes=64)
         nc.vector.tensor_copy(x0[:], word_table[0][:].bitcast(U32).indirect(offsets[:]))

@@ -106,79 +106,103 @@ def tile_picked_zrgcn_tanh_p_kernel(tc, x_words, x_scales, w0, w1, w2, w3, gate,
                 quantise(d, o, c0, c1)
 
         whole_scalar = [("scalar", 0, M)]
-        shared = [("vector", 0, 192), ("scalar", 192, M)]
+        shared = [("vector", 0, 160), ("scalar", 160, M)]
+        three = [("vector", 0, P), ("vector", P, 192), ("scalar", 192, M)]
         last = [("vector", 0, P), ("vector", P, M)]
 
         x0 = keep.tile([P, S], U32, name="x_codes0", align_bytes=64)
         nc.vector.tensor_copy(x0[:], word_table[0][:].bitcast(U32).indirect(offsets[:]))
+        x1 = keep.tile([P, S], U32, name="x_codes1", align_bytes=64)
+        nc.vector.tensor_copy(x1[:], word_table[1][:].bitcast(U32).indirect(offsets[:]))
         x_codes = {}
         for d in parts:
             x_codes[d, 0] = x0[:, d * V : (d + 1) * V]
-            x1 = keep.tile([P, V], U32, name="x_codes1_%d" % d, align_bytes=64)
-            nc.vector.tensor_copy(
-                x1[:], word_table[1][:].bitcast(U32).indirect(offsets[:, d * LIST_COLS : (d + 1) * LIST_COLS])
-            )
-            x_codes[d, 1] = x1[:]
+            x_codes[d, 1] = x1[:, d * V : (d + 1) * V]
 
         prepare(1, 0, whole_scalar, [(0, M)])
 
         def x_plane(d, o, c0, c1):
             return x_sc[4 * o : P, d * V + c0 : d * V + c1]
 
+        def transposed(y, d, o, h, c0, c1):
+            nc.tensor.matmul_mx(
+                out=y,
+                lhsT=x_codes[d, o][:, h * P : (h + 1) * P].bitcast(FP8X4),
+                lhsT_scale=x_plane(d, o, h * P, (h + 1) * P),
+                rhs=w_codes[d, o][:, c0:c1].bitcast(FP8X4),
+                rhs_scale=w_sc[d, o][:, c0:c1],
+                start=(o == 0),
+                stop=(o == PASSES - 1),
+            )
+
+        def turn(u, d, h, mt):
+            nc.tensor.matmul(
+                gated[mt][:, h * P : (h + 1) * P],
+                u,
+                ident[:],
+                is_transpose=True,
+                start=(d == 1 and h == 0),
+                stop=(d == D and h == HALVES - 1),
+            )
+
         gated = [psum.tile([P, V], F32, name="gated%d" % mt) for mt in range(HALVES)]
-        for d in (1, 2, 3):
+        for d in (1, 2):
             y = [psum2.tile([P, M], F32, name="y%d%d" % (d, h), tag="y%d" % h) for h in range(HALVES)]
             for o in range(PASSES):
                 if (d, o) != (1, 0):
-                    prepare(d, o, whole_scalar if d == 1 else shared, [(0, M)])
+                    prepare(d, o, [("vector", 0, M)] if (d, o) == (2, 1) else whole_scalar, [(0, M)])
+                for h in range(HALVES):
+                    transposed(y[h][:], d, o, h, 0, M)
+            for h in range(HALVES):
+                u = keep.tile([P, M], F32, name="u%d%d" % (d, h))
+                nc.scalar.activation(u[:], y[h][:], COPY, scale=gate_cols[:, d - 1, h : h + 1])
+                for mt in range(HALVES):
+                    turn(u[:, mt * P : (mt + 1) * P], d, h, mt)
+
+        y3 = {}
+        for mt in range(HALVES):
+            for h in range(HALVES):
+                y3[mt, h] = psum2.tile([P, P], F32, name="y3_%d%d" % (mt, h), tag="y%d" % h)
+        for o in range(PASSES):
+            if o == 0:
+                prepare(D, o, shared, [(0, M)])
+            else:
+                prepare(D, o, last, [(0, P), (P, M)])
+            for mt in range(HALVES):
+                for h in range(HALVES):
+                    transposed(y3[mt, h][:], D, o, h, mt * P, (mt + 1) * P)
+        for mt in range(HALVES):
+            for h in range(HALVES):
+                u = keep.tile([P, P], F32, name="u3_%d%d" % (mt, h))
+                nc.scalar.activation(u[:], y3[mt, h][:], COPY, scale=gate_cols[:, D - 1, h : h + 1])
+                turn(u[:], D, h, mt)
+
+        y0 = {}
+        for mt in range(HALVES):
+            y0[mt, 0] = psum.tile([P, P], F32, name="y0_%d0" % mt, tag="self%d" % mt)
+            y0[mt, 1] = psum2.tile([P, P], F32, name="y0_%d1" % mt, tag="y%d" % mt)
+        for o in range(PASSES):
+            prepare(0, o, last, [(0, P), (P, M)])
+            for mt in range(HALVES):
                 for h in range(HALVES):
                     nc.tensor.matmul_mx(
-                        out=y[h][:],
-                        lhsT=x_codes[d, o][:, h * P : (h + 1) * P].bitcast(FP8X4),
-                        lhsT_scale=x_plane(d, o, h * P, (h + 1) * P),
-                        rhs=w_codes[d, o][:].bitcast(FP8X4),
-                        rhs_scale=w_sc[d, o][:],
+                        out=y0[mt, h][:],
+                        lhsT=w_codes[0, o][:, mt * P : (mt + 1) * P].bitcast(FP8X4),
+                        lhsT_scale=w_sc[0, o][:, mt * P : (mt + 1) * P],
+                        rhs=x_codes[0, o][:, h * P : (h + 1) * P].bitcast(FP8X4),
+                        rhs_scale=x_plane(0, o, h * P, (h + 1) * P),
                         start=(o == 0),
                         stop=(o == PASSES - 1),
                     )
-            for h in range(HALVES):
-                u = keep.tile([P, M], F32, name="u%d%d" % (d, h))
-                g = gate_cols[:, d - 1, h : h + 1]
-                nc.scalar.activation(u[:], y[h][:], COPY, scale=g)
-                for mt in range(HALVES):
-                    nc.tensor.matmul(
-                        gated[mt][:, h * P : (h + 1) * P],
-                        u[:, mt * P : (mt + 1) * P],
-                        ident[:],
-                        is_transpose=True,
-                        start=(d == 1 and h == 0),
-                        stop=(d == D and h == HALVES - 1),
-                    )
-
-        y0 = [psum.tile([P, V], F32, name="y0_%d" % mt, tag="self%d" % mt) for mt in range(HALVES)]
-        for o in range(PASSES):
-            if o == 0:
-                prepare(0, o, shared, [(0, M)])
-            else:
-                prepare(0, o, last, [(0, P), (P, M)])
-            for mt in range(HALVES):
-                nc.tensor.matmul_mx(
-                    out=y0[mt][:],
-                    lhsT=w_codes[0, o][:, mt * P : (mt + 1) * P].bitcast(FP8X4),
-                    lhsT_scale=w_sc[0, o][:, mt * P : (mt + 1) * P],
-                    rhs=x_codes[0, o].bitcast(FP8X4),
-                    rhs_scale=x_plane(0, o, 0, V),
-                    start=(o == 0),
-                    stop=(o == PASSES - 1),
-                )
         sums = []
         for mt in range(HALVES):
             part = keep.tile([P, V], F32, name="part%d" % mt)
             nc.scalar.activation(part[:], gated[mt][:], COPY)
             sums.append(part)
         for mt in range(HALVES):
-            z = keep.tile([P, V], F32, name="z%d" % mt)
-            nc.vector.tensor_tensor(z[:], y0[mt][:], sums[mt][:], ADD)
             res = keep.tile([P, V], F32, name="res%d" % mt)
-            nc.scalar.activation(res[:], z[:], TANH)
+            for h in range(HALVES):
+                z = keep.tile([P, P], F32, name="z%d%d" % (mt, h))
+                nc.vector.tensor_tensor(z[:], y0[mt, h][:], sums[mt][:, h * P : (h + 1) * P], ADD)
+                nc.scalar.activation(res[:, h * P : (h + 1) * P], z[:], TANH)
             nc.sync.dma_start(out=out[mt * P : (mt + 1) * P, :], in_=res[:])

@@ -25,7 +25,7 @@ PASSES = K // K_PASS
 HALVES = 2
 LIST_COLS = V // 16
 VECTOR_COLS = 176
-HEAD = 384
+HEAD = 768
 
 
 def tile_picked_zrgcn_tanh_p_kernel(tc, x_words, x_scales, w0, w1, w2, w3, gate, offs, out):
@@ -43,8 +43,9 @@ def tile_picked_zrgcn_tanh_p_kernel(tc, x_words, x_scales, w0, w1, w2, w3, gate,
         gate_rows = keep.tile([P, D, P], F32, name="gate_rows")
         ident = keep.tile([P, P], F32, name="ident")
         nc.vector.memset(scale_table[:].bitcast(I32), 0)
-        make_identity(nc, ident[:])
-        nc.gpsimd.memset(gate_rows[:], 0.0)
+        nc.vector.memset(ident[:], 0.0)
+        nc.vector.memset(gate_rows[:], 0.0)
+        make_identity(nc, ident[:], nomemset=True)
 
         raw = {}
 
@@ -55,8 +56,8 @@ def tile_picked_zrgcn_tanh_p_kernel(tc, x_words, x_scales, w0, w1, w2, w3, gate,
 
         word_table = [keep.tile([P, T], I32, name="word_table%d" % o, align_bytes=64) for o in range(PASSES)]
         words = [x_words[o].rearrange("p n t -> p (n t)").bitcast(I32) for o in range(PASSES)]
-        nc.sync.dma_start(offsets[:], offs)
         nc.sync.dma_start(out=word_table[0][:, 0:HEAD], in_=words[0][:, 0:HEAD])
+        nc.sync.dma_start(offsets[:], offs)
         for q in range(4):
             nc.sync.dma_start(
                 out=scale_table[32 * q : 32 * q + 8, :].bitcast(I32),
@@ -146,18 +147,31 @@ def tile_picked_zrgcn_tanh_p_kernel(tc, x_words, x_scales, w0, w1, w2, w3, gate,
             )
 
         gated = [psum.tile([P, V], F32, name="gated%d" % mt) for mt in range(HALVES)]
+        y = {}
         for d in (1, 2):
-            y = [psum2.tile([P, M], F32, name="y%d%d" % (d, h), tag="y%d" % h) for h in range(HALVES)]
-            for o in range(PASSES):
-                if (d, o) != (1, 0):
-                    prepare(d, o, [("vector", 0, M)] if (d, o) == (2, 1) else whole_scalar, [(0, M)])
-                for h in range(HALVES):
-                    transposed(y[h][:], d, o, h, 0, M)
+            for h in range(HALVES):
+                y[d, h] = psum2.tile([P, M], F32, name="y%d%d" % (d, h), tag="y%d" % h)
+
+        def multiply(d, o):
+            for h in range(HALVES):
+                transposed(y[d, h][:], d, o, h, 0, M)
+
+        def leave(d):
             for h in range(HALVES):
                 u = keep.tile([P, M], F32, name="u%d%d" % (d, h))
-                nc.scalar.activation(u[:], y[h][:], COPY, scale=gate_cols[:, d - 1, h : h + 1])
+                nc.scalar.activation(u[:], y[d, h][:], COPY, scale=gate_cols[:, d - 1, h : h + 1])
                 for mt in range(HALVES):
                     turn(u[:, mt * P : (mt + 1) * P], d, h, mt)
+
+        multiply(1, 0)
+        prepare(1, 1, whole_scalar, [(0, M)])
+        multiply(1, 1)
+        prepare(2, 0, whole_scalar, [(0, M)])
+        multiply(2, 0)
+        prepare(2, 1, shared, [(0, M)])
+        leave(1)
+        multiply(2, 1)
+        leave(2)
 
         y3 = {}
         for mt in range(HALVES):
@@ -171,6 +185,7 @@ def tile_picked_zrgcn_tanh_p_kernel(tc, x_words, x_scales, w0, w1, w2, w3, gate,
             for mt in range(HALVES):
                 for h in range(HALVES):
                     transposed(y3[mt, h][:], D, o, h, mt * P, (mt + 1) * P)
+        prepare(0, 0, shared, [(0, P), (P, M)])
         for mt in range(HALVES):
             for h in range(HALVES):
                 u = keep.tile([P, P], F32, name="u3_%d%d" % (mt, h))
@@ -182,7 +197,8 @@ def tile_picked_zrgcn_tanh_p_kernel(tc, x_words, x_scales, w0, w1, w2, w3, gate,
             y0[mt, 0] = psum.tile([P, P], F32, name="y0_%d0" % mt, tag="self%d" % mt)
             y0[mt, 1] = psum2.tile([P, P], F32, name="y0_%d1" % mt, tag="y%d" % mt)
         for o in range(PASSES):
-            prepare(0, o, last, [(0, P), (P, M)])
+            if o == 1:
+                prepare(0, o, last, [(0, P), (P, M)])
             for mt in range(HALVES):
                 for h in range(HALVES):
                     nc.tensor.matmul_mx(

@@ -25,7 +25,7 @@ PASSES = K // K_PASS
 HALVES = 2
 LIST_COLS = V // 16
 VECTOR_COLS = 176
-HEAD = 768
+HEAD = 384
 
 
 def tile_picked_zrgcn_tanh_p_kernel(tc, x_words, x_scales, w0, w1, w2, w3, gate, offs, out):
@@ -43,14 +43,14 @@ def tile_picked_zrgcn_tanh_p_kernel(tc, x_words, x_scales, w0, w1, w2, w3, gate,
         gate_rows = keep.tile([P, D, P], F32, name="gate_rows")
         ident = keep.tile([P, P], F32, name="ident")
         nc.vector.memset(scale_table[:].bitcast(I32), 0)
-        nc.vector.memset(ident[:], 0.0)
         nc.vector.memset(gate_rows[:], 0.0)
+        nc.vector.memset(ident[:], 0.0)
         make_identity(nc, ident[:], nomemset=True)
 
         raw = {}
 
         def load_weight(d, o):
-            raw[d, o] = keep.tile([P, PACK, M], F32, name="raw%d%d" % (d, o), align_bytes=64)
+            raw[d, o] = keep.tile([P, PACK, M], F32, name="raw%d%d" % (d, o), tag="raw%d%d" % (d, o), align_bytes=64)
             rows = weights[d][o * K_PASS : (o + 1) * K_PASS, :]
             nc.sync.dma_start(out=raw[d, o][:], in_=rows.rearrange("(p j) m -> p j m", j=PACK))
 
@@ -58,14 +58,14 @@ def tile_picked_zrgcn_tanh_p_kernel(tc, x_words, x_scales, w0, w1, w2, w3, gate,
         words = [x_words[o].rearrange("p n t -> p (n t)").bitcast(I32) for o in range(PASSES)]
         nc.sync.dma_start(out=word_table[0][:, 0:HEAD], in_=words[0][:, 0:HEAD])
         nc.sync.dma_start(offsets[:], offs)
-        for q in range(4):
+        for q in (2, 3, 0, 1):
             nc.sync.dma_start(
                 out=scale_table[32 * q : 32 * q + 8, :].bitcast(I32),
                 in_=x_scales[:, 4 * q : 4 * q + 4, :].bitcast(I32),
             )
+        nc.sync.dma_start(out=gate_rows[0:HALVES, :, :], in_=gate[:, 0, :].rearrange("d (h c) -> h d c", h=HALVES))
         nc.sync.dma_start(out=word_table[0][:, HEAD:T], in_=words[0][:, HEAD:T])
         nc.sync.dma_start(out=word_table[1][:], in_=words[1])
-        nc.sync.dma_start(out=gate_rows[0:HALVES, :, :], in_=gate[:, 0, :].rearrange("d (h c) -> h d c", h=HALVES))
         for d in parts:
             for o in range(PASSES):
                 if (d, o) not in raw:
@@ -156,12 +156,12 @@ def tile_picked_zrgcn_tanh_p_kernel(tc, x_words, x_scales, w0, w1, w2, w3, gate,
             for h in range(HALVES):
                 transposed(y[d, h][:], d, o, h, 0, M)
 
-        def leave(d):
+        def leave(d, slot):
+            u = keep.tile([P, HALVES, M], F32, name="u%d" % d, tag=slot, align_bytes=64)
             for h in range(HALVES):
-                u = keep.tile([P, M], F32, name="u%d%d" % (d, h))
-                nc.scalar.activation(u[:], y[d, h][:], COPY, scale=gate_cols[:, d - 1, h : h + 1])
+                nc.scalar.activation(u[:, h, :], y[d, h][:], COPY, scale=gate_cols[:, d - 1, h : h + 1])
                 for mt in range(HALVES):
-                    turn(u[:, mt * P : (mt + 1) * P], d, h, mt)
+                    turn(u[:, h, mt * P : (mt + 1) * P], d, h, mt)
 
         multiply(1, 0)
         prepare(1, 1, whole_scalar, [(0, M)])
@@ -169,28 +169,28 @@ def tile_picked_zrgcn_tanh_p_kernel(tc, x_words, x_scales, w0, w1, w2, w3, gate,
         prepare(2, 0, whole_scalar, [(0, M)])
         multiply(2, 0)
         prepare(2, 1, shared, [(0, M)])
-        leave(1)
+        leave(1, "raw21")
         multiply(2, 1)
-        leave(2)
 
         y3 = {}
-        for mt in range(HALVES):
-            for h in range(HALVES):
-                y3[mt, h] = psum2.tile([P, P], F32, name="y3_%d%d" % (mt, h), tag="y%d" % h)
         for o in range(PASSES):
             if o == 0:
                 prepare(D, o, shared, [(0, M)])
+                leave(2, "raw30")
+                for mt in range(HALVES):
+                    for h in range(HALVES):
+                        y3[mt, h] = psum2.tile([P, P], F32, name="y3_%d%d" % (mt, h), tag="y%d" % h)
             else:
                 prepare(D, o, last, [(0, P), (P, M)])
             for mt in range(HALVES):
                 for h in range(HALVES):
                     transposed(y3[mt, h][:], D, o, h, mt * P, (mt + 1) * P)
         prepare(0, 0, shared, [(0, P), (P, M)])
+        u3 = keep.tile([P, HALVES, HALVES, P], F32, name="u3", tag="raw00", align_bytes=64)
         for mt in range(HALVES):
             for h in range(HALVES):
-                u = keep.tile([P, P], F32, name="u3_%d%d" % (mt, h))
-                nc.scalar.activation(u[:], y3[mt, h][:], COPY, scale=gate_cols[:, D - 1, h : h + 1])
-                turn(u[:], D, h, mt)
+                nc.scalar.activation(u3[:, mt, h, :], y3[mt, h][:], COPY, scale=gate_cols[:, D - 1, h : h + 1])
+                turn(u3[:, mt, h, :], D, h, mt)
 
         y0 = {}
         for mt in range(HALVES):

@@ -15,7 +15,6 @@ U8 = mybir.dt.uint8
 FP8X4 = mybir.dt.float8_e4m3fn_x4
 COPY = mybir.ActivationFunctionType.Copy
 TANH = mybir.ActivationFunctionType.Tanh
-MULT = mybir.AluOpType.mult
 ADD = mybir.AluOpType.add
 
 P = 128
@@ -23,9 +22,11 @@ PACK = 4
 K_PASS = P * PACK
 PASSES = K // K_PASS
 HALVES = 2
-LIST_COLS = V // 16
-VECTOR_COLS = 176
 HEAD = 384
+KB = 1024
+AT_RAW = {(1, 1): 0, (0, 1): 0, (2, 0): 4 * KB, (2, 1): 10 * KB, (3, 0): 14 * KB, (3, 1): 18 * KB, (1, 0): 20 * KB, (0, 0): 22 * KB}
+AT_SCALES = 3 * KB
+AT_TABLE0 = 10 * KB
 
 
 def tile_picked_zrgcn_tanh_p_kernel(tc, x_words, x_scales, w0, w1, w2, w3, gate, offs, out):
@@ -35,41 +36,42 @@ def tile_picked_zrgcn_tanh_p_kernel(tc, x_words, x_scales, w0, w1, w2, w3, gate,
 
     with ExitStack() as ctx:
         keep = ctx.enter_context(tc.tile_pool(name="keep", bufs=1))
+        reuse = ctx.enter_context(tc.tile_pool(name="reuse", bufs=1))
         psum = ctx.enter_context(tc.psum_pool(name="psum", bufs=1))
         psum2 = ctx.enter_context(tc.psum_pool(name="psum2", bufs=2))
 
+        def tile_at(shape, dtype, name, at):
+            if at is None:
+                return keep.tile(shape, dtype, name=name, align_bytes=64)
+            return reuse.tile(shape, dtype, name=name, align_bytes=64, offset=at)
+
         offsets = keep.tile([P, S // 16], U16, name="offsets")
-        scale_table = keep.tile([P, T], U8, name="scale_table", align_bytes=64)
-        gate_rows = keep.tile([P, D, P], F32, name="gate_rows")
+        scale_table = tile_at([P, T], U8, "scale_table", AT_SCALES)
+        gate_rows = tile_at([P, D, P], F32, "gate_rows", None)
         ident = keep.tile([P, P], F32, name="ident")
         nc.vector.memset(scale_table[:].bitcast(I32), 0)
         nc.vector.memset(gate_rows[:], 0.0)
         nc.vector.memset(ident[:], 0.0)
+        x_sc = tile_at([P, S], U8, "x_sc", None)
+        nc.vector.memset(x_sc[:].bitcast(I32), 0)
         make_identity(nc, ident[:], nomemset=True)
 
         raw = {}
 
         def load_weight(d, o):
-            raw[d, o] = keep.tile([P, PACK, M], F32, name="raw%d%d" % (d, o), tag="raw%d%d" % (d, o), align_bytes=64)
+            raw[d, o] = tile_at([P, PACK, M], F32, "raw%d%d" % (d, o), AT_RAW.get((d, o)))
             rows = weights[d][o * K_PASS : (o + 1) * K_PASS, :]
             nc.sync.dma_start(out=raw[d, o][:], in_=rows.rearrange("(p j) m -> p j m", j=PACK))
 
-        word_table = [keep.tile([P, T], I32, name="word_table%d" % o, align_bytes=64) for o in range(PASSES)]
+        word_table = [tile_at([P, T], I32, "word_table0", AT_TABLE0), tile_at([P, T], I32, "word_table1", None)]
         words = [x_words[o].rearrange("p n t -> p (n t)").bitcast(I32) for o in range(PASSES)]
         nc.sync.dma_start(out=word_table[0][:, 0:HEAD], in_=words[0][:, 0:HEAD])
         nc.sync.dma_start(offsets[:], offs)
-        for q in (2, 3, 0, 1):
-            nc.sync.dma_start(
-                out=scale_table[32 * q : 32 * q + 8, :].bitcast(I32),
-                in_=x_scales[:, 4 * q : 4 * q + 4, :].bitcast(I32),
-            )
-        nc.sync.dma_start(out=gate_rows[0:HALVES, :, :], in_=gate[:, 0, :].rearrange("d (h c) -> h d c", h=HALVES))
+        nc.sync.dma_start(out=scale_table[0:P:4, :].bitcast(I32), in_=x_scales.rearrange("o q n -> q o n").bitcast(I32))
         nc.sync.dma_start(out=word_table[0][:, HEAD:T], in_=words[0][:, HEAD:T])
+        nc.sync.dma_start(out=gate_rows[0:HALVES, :, :], in_=gate[:, 0, :].rearrange("d (h c) -> h d c", h=HALVES))
         nc.sync.dma_start(out=word_table[1][:], in_=words[1])
-        for d in parts:
-            for o in range(PASSES):
-                if (d, o) not in raw:
-                    load_weight(d, o)
+        load_weight(1, 0)
 
         gate_ps = psum.tile([P, D, P], F32, name="gate_ps", tag="self1")
         for d in range(D):
@@ -77,8 +79,20 @@ def tile_picked_zrgcn_tanh_p_kernel(tc, x_words, x_scales, w0, w1, w2, w3, gate,
         gate_cols = keep.tile([P, D, HALVES], F32, name="gate_cols")
         nc.scalar.activation(gate_cols[:], gate_ps[:, :, 0:HALVES], COPY)
 
-        x_sc = keep.tile([P, S], U8, name="x_sc", align_bytes=64)
-        nc.vector.tensor_copy(x_sc[:], scale_table[:].indirect(offsets[:]))
+        picked_sc = tile_at([P, S], U8, "picked_sc", None)
+        nc.vector.tensor_copy(picked_sc[:], scale_table[:].indirect(offsets[:]))
+
+        def place_scales(o):
+            for r in range(4):
+                nc.sync.dma_start(
+                    out=x_sc[4 * o + r : P : 32, :].bitcast(I32),
+                    in_=picked_sc[4 * o + 8 * r : P : 32, :].bitcast(I32),
+                )
+
+        place_scales(0)
+        load_weight(1, 1)
+        load_weight(2, 0)
+        place_scales(1)
 
         w_codes, w_sc, grouped = {}, {}, {}
 
@@ -98,7 +112,7 @@ def tile_picked_zrgcn_tanh_p_kernel(tc, x_words, x_scales, w0, w1, w2, w3, gate,
             )
 
         def prepare(d, o, plan, cuts):
-            grouped[d, o] = keep.tile([P, M, PACK], BF16, name="grouped%d%d" % (d, o), align_bytes=64)
+            grouped[d, o] = tile_at([P, M, PACK], BF16, "grouped%d%d" % (d, o), None)
             w_codes[d, o] = keep.tile([P, M], U32, name="w_codes%d%d" % (d, o), align_bytes=64)
             w_sc[d, o] = keep.tile([P, M], U8, name="w_sc%d%d" % (d, o), align_bytes=64)
             for engine, c0, c1 in plan:
@@ -108,11 +122,12 @@ def tile_picked_zrgcn_tanh_p_kernel(tc, x_words, x_scales, w0, w1, w2, w3, gate,
 
         whole_scalar = [("scalar", 0, M)]
         shared = [("vector", 0, 160), ("scalar", 160, M)]
-        three = [("vector", 0, P), ("vector", P, 192), ("scalar", 192, M)]
         last = [("vector", 0, P), ("vector", P, M)]
 
         x0 = keep.tile([P, S], U32, name="x_codes0", align_bytes=64)
         nc.vector.tensor_copy(x0[:], word_table[0][:].bitcast(U32).indirect(offsets[:]))
+        load_weight(2, 1)
+        load_weight(D, 0)
         x1 = keep.tile([P, S], U32, name="x_codes1", align_bytes=64)
         nc.vector.tensor_copy(x1[:], word_table[1][:].bitcast(U32).indirect(offsets[:]))
         x_codes = {}
@@ -157,26 +172,29 @@ def tile_picked_zrgcn_tanh_p_kernel(tc, x_words, x_scales, w0, w1, w2, w3, gate,
                 transposed(y[d, h][:], d, o, h, 0, M)
 
         def leave(d, slot):
-            u = keep.tile([P, HALVES, M], F32, name="u%d" % d, tag=slot, align_bytes=64)
+            u = tile_at([P, HALVES, M], F32, "u%d" % d, slot)
             for h in range(HALVES):
                 nc.scalar.activation(u[:, h, :], y[d, h][:], COPY, scale=gate_cols[:, d - 1, h : h + 1])
                 for mt in range(HALVES):
                     turn(u[:, h, mt * P : (mt + 1) * P], d, h, mt)
 
+        load_weight(D, 1)
+        load_weight(0, 0)
         multiply(1, 0)
         prepare(1, 1, whole_scalar, [(0, M)])
+        load_weight(0, 1)
         multiply(1, 1)
         prepare(2, 0, whole_scalar, [(0, M)])
         multiply(2, 0)
         prepare(2, 1, shared, [(0, M)])
-        leave(1, "raw21")
+        leave(1, AT_RAW[2, 1])
         multiply(2, 1)
 
         y3 = {}
         for o in range(PASSES):
             if o == 0:
                 prepare(D, o, shared, [(0, M)])
-                leave(2, "raw30")
+                leave(2, AT_RAW[3, 0])
                 for mt in range(HALVES):
                     for h in range(HALVES):
                         y3[mt, h] = psum2.tile([P, P], F32, name="y3_%d%d" % (mt, h), tag="y%d" % h)
@@ -186,7 +204,7 @@ def tile_picked_zrgcn_tanh_p_kernel(tc, x_words, x_scales, w0, w1, w2, w3, gate,
                 for h in range(HALVES):
                     transposed(y3[mt, h][:], D, o, h, mt * P, (mt + 1) * P)
         prepare(0, 0, shared, [(0, P), (P, M)])
-        u3 = keep.tile([P, HALVES, HALVES, P], F32, name="u3", tag="raw00", align_bytes=64)
+        u3 = tile_at([P, HALVES, HALVES, P], F32, "u3", AT_RAW[0, 0])
         for mt in range(HALVES):
             for h in range(HALVES):
                 nc.scalar.activation(u3[:, mt, h, :], y3[mt, h][:], COPY, scale=gate_cols[:, D - 1, h : h + 1])

@@ -25,7 +25,7 @@ HALVES = 2
 HEAD = 384
 KB = 1024
 AT_RAW = {(1, 1): 0, (0, 1): 0, (2, 0): 4 * KB, (2, 1): 10 * KB, (3, 0): 14 * KB, (3, 1): 18 * KB, (1, 0): 20 * KB, (0, 0): 22 * KB}
-AT_SCALES = 3 * KB
+AT_PICKED = 4 * KB - 512
 AT_TABLE0 = 10 * KB
 
 
@@ -46,14 +46,12 @@ def tile_picked_zrgcn_tanh_p_kernel(tc, x_words, x_scales, w0, w1, w2, w3, gate,
             return reuse.tile(shape, dtype, name=name, align_bytes=64, offset=at)
 
         offsets = keep.tile([P, S // 16], U16, name="offsets")
-        scale_table = tile_at([P, T], U8, "scale_table", AT_SCALES)
+        scale_table = tile_at([P, T], U8, "scale_table", None)
         gate_rows = tile_at([P, D, P], F32, "gate_rows", None)
         ident = keep.tile([P, P], F32, name="ident")
         nc.vector.memset(scale_table[:].bitcast(I32), 0)
         nc.vector.memset(gate_rows[:], 0.0)
         nc.vector.memset(ident[:], 0.0)
-        x_sc = tile_at([P, S], U8, "x_sc", None)
-        nc.vector.memset(x_sc[:].bitcast(I32), 0)
         make_identity(nc, ident[:], nomemset=True)
 
         raw = {}
@@ -79,20 +77,23 @@ def tile_picked_zrgcn_tanh_p_kernel(tc, x_words, x_scales, w0, w1, w2, w3, gate,
         gate_cols = keep.tile([P, D, HALVES], F32, name="gate_cols")
         nc.scalar.activation(gate_cols[:], gate_ps[:, :, 0:HALVES], COPY)
 
-        picked_sc = tile_at([P, S], U8, "picked_sc", None)
+        picked_sc = tile_at([P, S], U8, "picked_sc", AT_PICKED)
         nc.vector.tensor_copy(picked_sc[:], scale_table[:].indirect(offsets[:]))
+        x_sc = tile_at([P, S], U8, "x_sc", None)
+        nc.vector.tensor_copy(x_sc[:].bitcast(I32), picked_sc[:].bitcast(I32))
+        moves = [(o, r) for o in range(PASSES) for r in range(1, 4)]
 
-        def place_scales(o):
-            for r in range(4):
-                nc.sync.dma_start(
-                    out=x_sc[4 * o + r : P : 32, :].bitcast(I32),
-                    in_=picked_sc[4 * o + 8 * r : P : 32, :].bitcast(I32),
-                )
+        def place_scales(o, r):
+            nc.sync.dma_start(
+                out=x_sc[4 * o + r : P : 32, :].bitcast(I32),
+                in_=x_sc[4 * o + 8 * r : P : 32, :].bitcast(I32),
+            )
 
-        place_scales(0)
+        place_scales(*moves[0])
         load_weight(1, 1)
         load_weight(2, 0)
-        place_scales(1)
+        for move in moves[1:]:
+            place_scales(*move)
 
         w_codes, w_sc, grouped = {}, {}, {}
 

@@ -24,15 +24,16 @@ PASSES = K // K_PASS
 HALVES = 2
 HEAD = 384
 KB = 1024
-AT_RAW = {(1, 1): 0, (0, 1): 0, (2, 0): 4 * KB, (2, 1): 10 * KB, (3, 0): 14 * KB, (3, 1): 18 * KB, (1, 0): 20 * KB, (0, 0): 22 * KB}
+VECTOR_COLS = 160
+AT_RAW = {(1, 1): 0, (2, 0): 4 * KB, (2, 1): 10 * KB, (3, 0): 14 * KB, (3, 1): 18 * KB, (1, 0): 30 * KB, (0, 0): 22 * KB, (0, 1): 26 * KB}
+SPLIT = {(0, 1): P}
 AT_PICKED = 4 * KB - 512
-AT_TABLE0 = 10 * KB
+AT_WORDS = [11 * KB, 22 * KB]
 
 
 def tile_picked_zrgcn_tanh_p_kernel(tc, x_words, x_scales, w0, w1, w2, w3, gate, offs, out):
     nc = tc.nc
     weights = [w0, w1, w2, w3]
-    parts = [1, 2, 3, 0]
 
     with ExitStack() as ctx:
         keep = ctx.enter_context(tc.tile_pool(name="keep", bufs=1))
@@ -41,13 +42,12 @@ def tile_picked_zrgcn_tanh_p_kernel(tc, x_words, x_scales, w0, w1, w2, w3, gate,
         psum2 = ctx.enter_context(tc.psum_pool(name="psum2", bufs=2))
 
         def tile_at(shape, dtype, name, at):
-            if at is None:
-                return keep.tile(shape, dtype, name=name, align_bytes=64)
             return reuse.tile(shape, dtype, name=name, align_bytes=64, offset=at)
 
         offsets = keep.tile([P, S // 16], U16, name="offsets")
-        scale_table = tile_at([P, T], U8, "scale_table", None)
-        gate_rows = tile_at([P, D, P], F32, "gate_rows", None)
+        scale_table = keep.tile([P, T], U8, name="scale_table", align_bytes=64)
+        planes = keep.tile([P, S], U8, name="planes", align_bytes=64)
+        gate_rows = keep.tile([P, D, P], F32, name="gate_rows")
         ident = keep.tile([P, P], F32, name="ident")
         nc.vector.memset(scale_table[:].bitcast(I32), 0)
         nc.vector.memset(gate_rows[:], 0.0)
@@ -57,11 +57,16 @@ def tile_picked_zrgcn_tanh_p_kernel(tc, x_words, x_scales, w0, w1, w2, w3, gate,
         raw = {}
 
         def load_weight(d, o):
-            raw[d, o] = tile_at([P, PACK, M], F32, "raw%d%d" % (d, o), AT_RAW.get((d, o)))
-            rows = weights[d][o * K_PASS : (o + 1) * K_PASS, :]
-            nc.sync.dma_start(out=raw[d, o][:], in_=rows.rearrange("(p j) m -> p j m", j=PACK))
+            rows = weights[d][o * K_PASS : (o + 1) * K_PASS, :].rearrange("(p j) m -> p j m", j=PACK)
+            cut = SPLIT.get((d, o), M)
+            raw[d, o] = []
+            for c0, c1 in [(0, cut), (cut, M)]:
+                if c1 > c0:
+                    piece = tile_at([P, PACK, c1 - c0], F32, "raw%d%d_%d" % (d, o, c0), AT_RAW[d, o] + c0 * PACK * 4)
+                    nc.sync.dma_start(out=piece[:], in_=rows[:, :, c0:c1])
+                    raw[d, o].append((c0, c1, piece))
 
-        word_table = [tile_at([P, T], I32, "word_table0", AT_TABLE0), tile_at([P, T], I32, "word_table1", None)]
+        word_table = [tile_at([P, T], I32, "word_table%d" % o, AT_WORDS[o]) for o in range(PASSES)]
         words = [x_words[o].rearrange("p n t -> p (n t)").bitcast(I32) for o in range(PASSES)]
         nc.sync.dma_start(out=word_table[0][:, 0:HEAD], in_=words[0][:, 0:HEAD])
         nc.sync.dma_start(offsets[:], offs)
@@ -77,80 +82,78 @@ def tile_picked_zrgcn_tanh_p_kernel(tc, x_words, x_scales, w0, w1, w2, w3, gate,
         gate_cols = keep.tile([P, D, HALVES], F32, name="gate_cols")
         nc.scalar.activation(gate_cols[:], gate_ps[:, :, 0:HALVES], COPY)
 
-        picked_sc = tile_at([P, S], U8, "picked_sc", AT_PICKED)
-        nc.vector.tensor_copy(picked_sc[:], scale_table[:].indirect(offsets[:]))
-        x_sc = tile_at([P, S], U8, "x_sc", None)
-        nc.vector.tensor_copy(x_sc[:].bitcast(I32), picked_sc[:].bitcast(I32))
+        picked = tile_at([P, S], U8, "picked", AT_PICKED)
+        nc.vector.tensor_copy(picked[:], scale_table[:].indirect(offsets[:]))
+        nc.vector.tensor_copy(planes[:].bitcast(I32), picked[:].bitcast(I32))
         moves = [(o, r) for o in range(PASSES) for r in range(1, 4)]
 
-        def place_scales(o, r):
-            nc.sync.dma_start(
-                out=x_sc[4 * o + r : P : 32, :].bitcast(I32),
-                in_=x_sc[4 * o + 8 * r : P : 32, :].bitcast(I32),
-            )
+        def place_scales(some):
+            for o, r in some:
+                nc.sync.dma_start(
+                    out=planes[4 * o + r : P : 32, :].bitcast(I32),
+                    in_=planes[4 * o + 8 * r : P : 32, :].bitcast(I32),
+                )
 
-        place_scales(*moves[0])
+        place_scales(moves[:1])
         load_weight(1, 1)
         load_weight(2, 0)
-        for move in moves[1:]:
-            place_scales(*move)
+        place_scales(moves[1:])
 
-        w_codes, w_sc, grouped = {}, {}, {}
+        x_codes = []
+        for o in range(PASSES):
+            codes = keep.tile([P, S], U32, name="x_codes%d" % o, align_bytes=64)
+            nc.vector.tensor_copy(codes[:], word_table[o][:].bitcast(U32).indirect(offsets[:]))
+            x_codes.append(codes)
+        for d, o in [(2, 1), (3, 0), (3, 1), (0, 0), (0, 1)]:
+            load_weight(d, o)
 
-        def cast(d, o, engine, c0, c1):
-            dst = grouped[d, o][:, c0:c1, :].rearrange("p (c i) t -> p c t i", i=4)
-            src = raw[d, o][:, :, c0:c1].rearrange("p t (c i) -> p c t i", i=4)
-            if engine == "vector":
-                nc.vector.tensor_copy(out=dst, in_=src)
-            else:
-                nc.scalar.activation(dst, src, COPY)
-
-        def quantise(d, o, c0, c1):
-            nc.vector.quantize_mx(
-                out=w_codes[d, o][:, c0:c1].bitcast(FP8X4),
-                scales=w_sc[d, o][:, c0:c1],
-                in_=grouped[d, o][:, c0:c1, :].rearrange("p c t -> p (c t)"),
-            )
+        w_codes, w_scales = {}, {}
 
         def prepare(d, o, plan, cuts):
-            grouped[d, o] = tile_at([P, M, PACK], BF16, "grouped%d%d" % (d, o), None)
+            grouped = keep.tile([P, M, PACK], BF16, name="grouped%d%d" % (d, o), align_bytes=64)
             w_codes[d, o] = keep.tile([P, M], U32, name="w_codes%d%d" % (d, o), align_bytes=64)
-            w_sc[d, o] = keep.tile([P, M], U8, name="w_sc%d%d" % (d, o), align_bytes=64)
+            w_scales[d, o] = keep.tile([P, M], U8, name="w_scales%d%d" % (d, o), align_bytes=64)
+            dst = grouped[:].rearrange("p (c i) t -> p c t i", i=4)
             for engine, c0, c1 in plan:
-                cast(d, o, engine, c0, c1)
+                first, piece = [(a, t) for a, b, t in raw[d, o] if a <= c0 and c1 <= b][0]
+                src = piece[:, :, c0 - first : c1 - first].rearrange("p t (c i) -> p c t i", i=4)
+                if engine == "v":
+                    nc.vector.tensor_copy(out=dst[:, c0 // 4 : c1 // 4], in_=src)
+                else:
+                    nc.scalar.activation(dst[:, c0 // 4 : c1 // 4], src, COPY)
             for c0, c1 in cuts:
-                quantise(d, o, c0, c1)
+                nc.vector.quantize_mx(
+                    out=w_codes[d, o][:, c0:c1].bitcast(FP8X4),
+                    scales=w_scales[d, o][:, c0:c1],
+                    in_=grouped[:, c0:c1, :].rearrange("p c t -> p (c t)"),
+                )
 
-        whole_scalar = [("scalar", 0, M)]
-        shared = [("vector", 0, 160), ("scalar", 160, M)]
-        last = [("vector", 0, P), ("vector", P, M)]
+        def x_operand(d, o, c0, c1):
+            cols = slice(d * V + c0, d * V + c1)
+            return x_codes[o][:, cols].bitcast(FP8X4), planes[4 * o : P, cols]
 
-        x0 = keep.tile([P, S], U32, name="x_codes0", align_bytes=64)
-        nc.vector.tensor_copy(x0[:], word_table[0][:].bitcast(U32).indirect(offsets[:]))
-        load_weight(2, 1)
-        load_weight(D, 0)
-        x1 = keep.tile([P, S], U32, name="x_codes1", align_bytes=64)
-        nc.vector.tensor_copy(x1[:], word_table[1][:].bitcast(U32).indirect(offsets[:]))
-        x_codes = {}
-        for d in parts:
-            x_codes[d, 0] = x0[:, d * V : (d + 1) * V]
-            x_codes[d, 1] = x1[:, d * V : (d + 1) * V]
+        def w_operand(d, o, c0, c1):
+            return w_codes[d, o][:, c0:c1].bitcast(FP8X4), w_scales[d, o][:, c0:c1]
 
-        prepare(1, 0, whole_scalar, [(0, M)])
-
-        def x_plane(d, o, c0, c1):
-            return x_sc[4 * o : P, d * V + c0 : d * V + c1]
-
-        def transposed(y, d, o, h, c0, c1):
+        def multiply(y, stationary, moving, o):
             nc.tensor.matmul_mx(
                 out=y,
-                lhsT=x_codes[d, o][:, h * P : (h + 1) * P].bitcast(FP8X4),
-                lhsT_scale=x_plane(d, o, h * P, (h + 1) * P),
-                rhs=w_codes[d, o][:, c0:c1].bitcast(FP8X4),
-                rhs_scale=w_sc[d, o][:, c0:c1],
+                lhsT=stationary[0],
+                lhsT_scale=stationary[1],
+                rhs=moving[0],
+                rhs_scale=moving[1],
                 start=(o == 0),
                 stop=(o == PASSES - 1),
             )
+
+        gated = [psum.tile([P, V], F32, name="gated%d" % mt) for mt in range(HALVES)]
+        y = {}
+
+        def gated_pass(d, o):
+            for h in range(HALVES):
+                if o == 0:
+                    y[d, h] = psum2.tile([P, M], F32, name="y%d%d" % (d, h), tag="y%d" % h)
+                multiply(y[d, h][:], x_operand(d, o, h * P, (h + 1) * P), w_operand(d, o, 0, M), o)
 
         def turn(u, d, h, mt):
             nc.tensor.matmul(
@@ -162,82 +165,62 @@ def tile_picked_zrgcn_tanh_p_kernel(tc, x_words, x_scales, w0, w1, w2, w3, gate,
                 stop=(d == D and h == HALVES - 1),
             )
 
-        gated = [psum.tile([P, V], F32, name="gated%d" % mt) for mt in range(HALVES)]
-        y = {}
-        for d in (1, 2):
-            for h in range(HALVES):
-                y[d, h] = psum2.tile([P, M], F32, name="y%d%d" % (d, h), tag="y%d" % h)
-
-        def multiply(d, o):
-            for h in range(HALVES):
-                transposed(y[d, h][:], d, o, h, 0, M)
-
-        def leave(d, slot):
-            u = tile_at([P, HALVES, M], F32, "u%d" % d, slot)
+        def leave(d, at):
+            u = tile_at([P, HALVES, M], F32, "u%d" % d, at)
             for h in range(HALVES):
                 nc.scalar.activation(u[:, h, :], y[d, h][:], COPY, scale=gate_cols[:, d - 1, h : h + 1])
                 for mt in range(HALVES):
                     turn(u[:, h, mt * P : (mt + 1) * P], d, h, mt)
 
-        load_weight(D, 1)
-        load_weight(0, 0)
-        multiply(1, 0)
-        prepare(1, 1, whole_scalar, [(0, M)])
-        load_weight(0, 1)
-        multiply(1, 1)
-        prepare(2, 0, whole_scalar, [(0, M)])
-        multiply(2, 0)
-        prepare(2, 1, shared, [(0, M)])
-        leave(1, AT_RAW[2, 1])
-        multiply(2, 1)
-
+        whole = [(0, M)]
+        halves = [(0, P), (P, M)]
+        shared = [("v", 0, VECTOR_COLS), ("s", VECTOR_COLS, M)]
+        prepare(1, 0, [("s", 0, M)], whole)
+        gated_pass(1, 0)
+        for d, o in [(1, 1), (2, 0), (2, 1)]:
+            prepare(d, o, shared if (d, o) == (2, 1) else [("s", 0, M)], whole)
+            if (d, o) == (2, 1):
+                leave(1, AT_RAW[2, 1])
+            gated_pass(d, o)
+        prepare(3, 0, shared, whole)
+        leave(2, AT_RAW[3, 0])
+        quarters = [(mt, h) for mt in range(HALVES) for h in range(HALVES)]
         y3 = {}
-        for o in range(PASSES):
-            if o == 0:
-                prepare(D, o, shared, [(0, M)])
-                leave(2, AT_RAW[3, 0])
-                for mt in range(HALVES):
-                    for h in range(HALVES):
-                        y3[mt, h] = psum2.tile([P, P], F32, name="y3_%d%d" % (mt, h), tag="y%d" % h)
-            else:
-                prepare(D, o, last, [(0, P), (P, M)])
-            for mt in range(HALVES):
-                for h in range(HALVES):
-                    transposed(y3[mt, h][:], D, o, h, mt * P, (mt + 1) * P)
-        prepare(0, 0, shared, [(0, P), (P, M)])
+
+        def last_gated_pass(o):
+            for mt, h in quarters:
+                if o == 0:
+                    y3[mt, h] = psum2.tile([P, P], F32, name="y3_%d%d" % (mt, h), tag="y%d" % h)
+                multiply(y3[mt, h][:], x_operand(D, o, h * P, (h + 1) * P), w_operand(D, o, mt * P, (mt + 1) * P), o)
+
+        last_gated_pass(0)
+        prepare(3, 1, [("v", 0, P), ("v", P, M)], halves)
+        last_gated_pass(1)
+        prepare(0, 0, shared, halves)
         u3 = tile_at([P, HALVES, HALVES, P], F32, "u3", AT_RAW[0, 0])
-        for mt in range(HALVES):
-            for h in range(HALVES):
-                nc.scalar.activation(u3[:, mt, h, :], y3[mt, h][:], COPY, scale=gate_cols[:, D - 1, h : h + 1])
-                turn(u3[:, mt, h, :], D, h, mt)
+        for mt, h in quarters:
+            nc.scalar.activation(u3[:, mt, h, :], y3[mt, h][:], COPY, scale=gate_cols[:, D - 1, h : h + 1])
+            turn(u3[:, mt, h, :], D, h, mt)
 
         y0 = {}
         for mt in range(HALVES):
             y0[mt, 0] = psum.tile([P, P], F32, name="y0_%d0" % mt, tag="self%d" % mt)
             y0[mt, 1] = psum2.tile([P, P], F32, name="y0_%d1" % mt, tag="y%d" % mt)
-        for o in range(PASSES):
-            if o == 1:
-                prepare(0, o, last, [(0, P), (P, M)])
-            for mt in range(HALVES):
-                for h in range(HALVES):
-                    nc.tensor.matmul_mx(
-                        out=y0[mt, h][:],
-                        lhsT=w_codes[0, o][:, mt * P : (mt + 1) * P].bitcast(FP8X4),
-                        lhsT_scale=w_sc[0, o][:, mt * P : (mt + 1) * P],
-                        rhs=x_codes[0, o][:, h * P : (h + 1) * P].bitcast(FP8X4),
-                        rhs_scale=x_plane(0, o, h * P, (h + 1) * P),
-                        start=(o == 0),
-                        stop=(o == PASSES - 1),
-                    )
-        sums = []
+
+        def own_pass(o):
+            for mt, h in quarters:
+                multiply(y0[mt, h][:], w_operand(0, o, mt * P, (mt + 1) * P), x_operand(0, o, h * P, (h + 1) * P), o)
+
+        own_pass(0)
+        prepare(0, 1, [("v", 0, P), ("v", P, M)], halves)
+        sums = keep.tile([P, HALVES, V], F32, name="sums")
         for mt in range(HALVES):
-            part = keep.tile([P, V], F32, name="part%d" % mt)
-            nc.scalar.activation(part[:], gated[mt][:], COPY)
-            sums.append(part)
+            nc.scalar.activation(sums[:, mt, :], gated[mt][:], COPY)
+        own_pass(1)
         for mt in range(HALVES):
             res = keep.tile([P, V], F32, name="res%d" % mt)
             for h in range(HALVES):
                 z = keep.tile([P, P], F32, name="z%d%d" % (mt, h))
-                nc.vector.tensor_tensor(z[:], y0[mt, h][:], sums[mt][:, h * P : (h + 1) * P], ADD)
+                nc.vector.tensor_tensor(z[:], y0[mt, h][:], sums[:, mt, h * P : (h + 1) * P], ADD)
                 nc.scalar.activation(res[:, h * P : (h + 1) * P], z[:], TANH)
             nc.sync.dma_start(out=out[mt * P : (mt + 1) * P, :], in_=res[:])

@@ -24,9 +24,9 @@ PASSES = K // K_PASS
 HALVES = 2
 HEAD = 384
 KB = 1024
-VECTOR_COLS = 160
+VECTOR_COLS = 192
 AT_RAW = {(1, 1): 0, (2, 0): 4 * KB, (2, 1): 10 * KB, (3, 0): 14 * KB, (3, 1): 18 * KB, (1, 0): 30 * KB, (0, 0): 22 * KB, (0, 1): 26 * KB}
-SPLIT = {(0, 1): P}
+SPLIT = {}
 AT_PICKED = 4 * KB - 512
 AT_WORDS = [11 * KB, 22 * KB]
 
@@ -178,7 +178,7 @@ def tile_picked_zrgcn_tanh_p_kernel(tc, x_words, x_scales, w0, w1, w2, w3, gate,
         prepare(1, 0, [("s", 0, M)], whole)
         gated_pass(1, 0)
         for d, o in [(1, 1), (2, 0), (2, 1)]:
-            prepare(d, o, shared if (d, o) == (2, 1) else [("s", 0, M)], whole)
+            prepare(d, o, {(1, 1): [("s", 0, M)], (2, 0): [("v", 0, 128), ("s", 128, M)], (2, 1): shared}[d, o], whole)
             if (d, o) == (2, 1):
                 leave(1, AT_RAW[2, 1])
             gated_pass(d, o)
@@ -196,7 +196,7 @@ def tile_picked_zrgcn_tanh_p_kernel(tc, x_words, x_scales, w0, w1, w2, w3, gate,
         last_gated_pass(0)
         prepare(3, 1, [("v", 0, P), ("v", P, M)], halves)
         last_gated_pass(1)
-        prepare(0, 0, shared, halves)
+        prepare(0, 0, [("v", 0, 160), ("s", 160, M)], halves)
         u3 = tile_at([P, HALVES, HALVES, P], F32, "u3", AT_RAW[0, 0])
         for mt, h in quarters:
             nc.scalar.activation(u3[:, mt, h, :], y3[mt, h][:], COPY, scale=gate_cols[:, D - 1, h : h + 1])
@@ -212,8 +212,8 @@ def tile_picked_zrgcn_tanh_p_kernel(tc, x_words, x_scales, w0, w1, w2, w3, gate,
                 multiply(y0[mt, h][:], w_operand(0, o, mt * P, (mt + 1) * P), x_operand(0, o, h * P, (h + 1) * P), o)
 
         own_pass(0)
-        prepare(0, 1, [("v", 0, P), ("v", P, M)], halves)
-        sums = keep.tile([P, HALVES, V], F32, name="sums")
+        prepare(0, 1, [("v", 0, P), ("v", P, 192), ("s", 192, M)], halves)
+        sums = tile_at([P, HALVES, V], F32, "sums", AT_RAW[0, 1])
         for mt in range(HALVES):
             nc.scalar.activation(sums[:, mt, :], gated[mt][:], COPY)
         own_pass(1)

@@ -223,4 +223,5 @@ def tile_picked_zrgcn_tanh_p_kernel(tc, x_words, x_scales, w0, w1, w2, w3, gate,
                 z = keep.tile([P, P], F32, name="z%d%d" % (mt, h))
                 nc.vector.tensor_tensor(z[:], y0[mt, h][:], sums[:, mt, h * P : (h + 1) * P], ADD)
                 nc.scalar.activation(res[:, h * P : (h + 1) * P], z[:], TANH)
-            nc.sync.dma_start(out=out[mt * P : (mt + 1) * P, :], in_=res[:])
+            queue = nc.scalar if mt == HALVES - 1 else nc.sync
+            queue.dma_start(out=out[mt * P : (mt + 1) * P, :], in_=res[:])

@@ -113,14 +113,14 @@ def tile_picked_zrgcn_tanh_p_kernel(tc, x_words, x_scales, w0, w1, w2, w3, gate,
             grouped = keep.tile([P, M, PACK], BF16, name="grouped%d%d" % (d, o), align_bytes=64)
             w_codes[d, o] = keep.tile([P, M], U32, name="w_codes%d%d" % (d, o), align_bytes=64)
             w_scales[d, o] = keep.tile([P, M], U8, name="w_scales%d%d" % (d, o), align_bytes=64)
-            dst = grouped[:].rearrange("p (c i) t -> p c t i", i=4)
+            dst = grouped[:].rearrange("p (c i) t -> p c t i", i=2)
             for engine, c0, c1 in plan:
                 first, piece = [(a, t) for a, b, t in raw[d, o] if a <= c0 and c1 <= b][0]
-                src = piece[:, :, c0 - first : c1 - first].rearrange("p t (c i) -> p c t i", i=4)
+                src = piece[:, :, c0 - first : c1 - first].rearrange("p t (c i) -> p c t i", i=2)
                 if engine == "v":
-                    nc.vector.tensor_copy(out=dst[:, c0 // 4 : c1 // 4], in_=src)
+                    nc.vector.tensor_copy(out=dst[:, c0 // 2 : c1 // 2], in_=src)
                 else:
-                    nc.scalar.activation(dst[:, c0 // 4 : c1 // 4], src, COPY)
+                    nc.scalar.activation(dst[:, c0 // 2 : c1 // 2], src, COPY)
             for c0, c1 in cuts:
                 nc.vector.quantize_mx(
                     out=w_codes[d, o][:, c0:c1].bitcast(FP8X4),

from contextlib import ExitStack

import concourse.mybir as mybir
from concourse.masks import make_identity

K, T, S, V, D, M = 1024, 2048, 1024, 256, 3, 256
FLOPS = 2 * K * M * S

F32 = mybir.dt.float32
BF16 = mybir.dt.bfloat16
I32 = mybir.dt.int32
U32 = mybir.dt.uint32
U16 = mybir.dt.uint16
U8 = mybir.dt.uint8
FP8X4 = mybir.dt.float8_e4m3fn_x4
COPY = mybir.ActivationFunctionType.Copy
TANH = mybir.ActivationFunctionType.Tanh
ADD = mybir.AluOpType.add

P = 128
PACK = 4
K_PASS = P * PACK
PASSES = K // K_PASS
HALVES = 2
HEAD = 384
KB = 1024
VECTOR_COLS = 192
AT_RAW = {(1, 1): 0, (2, 0): 4 * KB, (2, 1): 10 * KB, (3, 0): 14 * KB, (3, 1): 18 * KB, (1, 0): 30 * KB, (0, 0): 22 * KB, (0, 1): 26 * KB}
SPLIT = {}
AT_PICKED = 4 * KB - 512
AT_WORDS = [11 * KB, 22 * KB]


def tile_picked_zrgcn_tanh_p_kernel(tc, x_words, x_scales, w0, w1, w2, w3, gate, offs, out):
    nc = tc.nc
    weights = [w0, w1, w2, w3]

    with ExitStack() as ctx:
        keep = ctx.enter_context(tc.tile_pool(name="keep", bufs=1))
        reuse = ctx.enter_context(tc.tile_pool(name="reuse", bufs=1))
        psum = ctx.enter_context(tc.psum_pool(name="psum", bufs=1))
        psum2 = ctx.enter_context(tc.psum_pool(name="psum2", bufs=2))

        def tile_at(shape, dtype, name, at):
            return reuse.tile(shape, dtype, name=name, align_bytes=64, offset=at)

        offsets = keep.tile([P, S // 16], U16, name="offsets")
        scale_table = keep.tile([P, T], U8, name="scale_table", align_bytes=64)
        planes = keep.tile([P, S], U8, name="planes", align_bytes=64)
        gate_rows = keep.tile([P, D, P], F32, name="gate_rows")
        ident = keep.tile([P, P], F32, name="ident")
        nc.vector.memset(scale_table[:].bitcast(I32), 0)
        nc.vector.memset(gate_rows[:], 0.0)
        nc.vector.memset(ident[:], 0.0)
        make_identity(nc, ident[:], nomemset=True)

        raw = {}

        def load_weight(d, o):
            rows = weights[d][o * K_PASS : (o + 1) * K_PASS, :].rearrange("(p j) m -> p j m", j=PACK)
            cut = SPLIT.get((d, o), M)
            raw[d, o] = []
            for c0, c1 in [(0, cut), (cut, M)]:
                if c1 > c0:
                    piece = tile_at([P, PACK, c1 - c0], F32, "raw%d%d_%d" % (d, o, c0), AT_RAW[d, o] + c0 * PACK * 4)
                    nc.sync.dma_start(out=piece[:], in_=rows[:, :, c0:c1])
                    raw[d, o].append((c0, c1, piece))

        word_table = [tile_at([P, T], I32, "word_table%d" % o, AT_WORDS[o]) for o in range(PASSES)]
        words = [x_words[o].rearrange("p n t -> p (n t)").bitcast(I32) for o in range(PASSES)]
        nc.sync.dma_start(out=word_table[0][:, 0:HEAD], in_=words[0][:, 0:HEAD])
        nc.sync.dma_start(offsets[:], offs)
        nc.sync.dma_start(out=scale_table[0:P:4, :].bitcast(I32), in_=x_scales.rearrange("o q n -> q o n").bitcast(I32))
        nc.sync.dma_start(out=word_table[0][:, HEAD:T], in_=words[0][:, HEAD:T])
        nc.sync.dma_start(out=gate_rows[0:HALVES, :, :], in_=gate[:, 0, :].rearrange("d (h c) -> h d c", h=HALVES))
        nc.sync.dma_start(out=word_table[1][:], in_=words[1])
        load_weight(1, 0)

        gate_ps = psum.tile([P, D, P], F32, name="gate_ps", tag="self1")
        for d in range(D):
            nc.tensor.transpose(gate_ps[:, d, :], gate_rows[:, d, :], ident[:])
        gate_cols = keep.tile([P, D, HALVES], F32, name="gate_cols")
        nc.scalar.activation(gate_cols[:], gate_ps[:, :, 0:HALVES], COPY)

        picked = tile_at([P, S], U8, "picked", AT_PICKED)
        nc.vector.tensor_copy(picked[:], scale_table[:].indirect(offsets[:]))
        nc.vector.tensor_copy(planes[:].bitcast(I32), picked[:].bitcast(I32))
        moves = [(o, r) for o in range(PASSES) for r in range(1, 4)]

        def place_scales(some):
            for o, r in some:
                nc.sync.dma_start(
                    out=planes[4 * o + r : P : 32, :].bitcast(I32),
                    in_=planes[4 * o + 8 * r : P : 32, :].bitcast(I32),
                )

        place_scales(moves[:1])
        load_weight(1, 1)
        load_weight(2, 0)
        place_scales(moves[1:])

        x_codes = []
        for o in range(PASSES):
            codes = keep.tile([P, S], U32, name="x_codes%d" % o, align_bytes=64)
            nc.vector.tensor_copy(codes[:], word_table[o][:].bitcast(U32).indirect(offsets[:]))
            x_codes.append(codes)
        for d, o in [(2, 1), (3, 0), (3, 1), (0, 0), (0, 1)]:
            load_weight(d, o)

        w_codes, w_scales = {}, {}

        def prepare(d, o, plan, cuts):
            grouped = keep.tile([P, M, PACK], BF16, name="grouped%d%d" % (d, o), align_bytes=64)
            w_codes[d, o] = keep.tile([P, M], U32, name="w_codes%d%d" % (d, o), align_bytes=64)
            w_scales[d, o] = keep.tile([P, M], U8, name="w_scales%d%d" % (d, o), align_bytes=64)
            dst = grouped[:].rearrange("p (c i) t -> p c t i", i=2)
            for engine, c0, c1 in plan:
                first, piece = [(a, t) for a, b, t in raw[d, o] if a <= c0 and c1 <= b][0]
                src = piece[:, :, c0 - first : c1 - first].rearrange("p t (c i) -> p c t i", i=2)
                if engine == "v":
                    nc.vector.tensor_copy(out=dst[:, c0 // 2 : c1 // 2], in_=src)
                else:
                    nc.scalar.activation(dst[:, c0 // 2 : c1 // 2], src, COPY)
            for c0, c1 in cuts:
                nc.vector.quantize_mx(
                    out=w_codes[d, o][:, c0:c1].bitcast(FP8X4),
                    scales=w_scales[d, o][:, c0:c1],
                    in_=grouped[:, c0:c1, :].rearrange("p c t -> p (c t)"),
                )

        def x_operand(d, o, c0, c1):
            cols = slice(d * V + c0, d * V + c1)
            return x_codes[o][:, cols].bitcast(FP8X4), planes[4 * o : P, cols]

        def w_operand(d, o, c0, c1):
            return w_codes[d, o][:, c0:c1].bitcast(FP8X4), w_scales[d, o][:, c0:c1]

        def multiply(y, stationary, moving, o):
            nc.tensor.matmul_mx(
                out=y,
                lhsT=stationary[0],
                lhsT_scale=stationary[1],
                rhs=moving[0],
                rhs_scale=moving[1],
                start=(o == 0),
                stop=(o == PASSES - 1),
            )

        gated = [psum.tile([P, V], F32, name="gated%d" % mt) for mt in range(HALVES)]
        y = {}

        def gated_pass(d, o):
            for h in range(HALVES):
                if o == 0:
                    y[d, h] = psum2.tile([P, M], F32, name="y%d%d" % (d, h), tag="y%d" % h)
                multiply(y[d, h][:], x_operand(d, o, h * P, (h + 1) * P), w_operand(d, o, 0, M), o)

        def turn(u, d, h, mt):
            nc.tensor.matmul(
                gated[mt][:, h * P : (h + 1) * P],
                u,
                ident[:],
                is_transpose=True,
                start=(d == 1 and h == 0),
                stop=(d == D and h == HALVES - 1),
            )

        def leave(d, at):
            u = tile_at([P, HALVES, M], F32, "u%d" % d, at)
            for h in range(HALVES):
                nc.scalar.activation(u[:, h, :], y[d, h][:], COPY, scale=gate_cols[:, d - 1, h : h + 1])
                for mt in range(HALVES):
                    turn(u[:, h, mt * P : (mt + 1) * P], d, h, mt)

        whole = [(0, M)]
        halves = [(0, P), (P, M)]
        shared = [("v", 0, VECTOR_COLS), ("s", VECTOR_COLS, M)]
        prepare(1, 0, [("s", 0, M)], whole)
        gated_pass(1, 0)
        for d, o in [(1, 1), (2, 0), (2, 1)]:
            prepare(d, o, {(1, 1): [("s", 0, M)], (2, 0): [("v", 0, 128), ("s", 128, M)], (2, 1): shared}[d, o], whole)
            if (d, o) == (2, 1):
                leave(1, AT_RAW[2, 1])
            gated_pass(d, o)
        prepare(3, 0, shared, whole)
        leave(2, AT_RAW[3, 0])
        quarters = [(mt, h) for mt in range(HALVES) for h in range(HALVES)]
        y3 = {}

        def last_gated_pass(o):
            for mt, h in quarters:
                if o == 0:
                    y3[mt, h] = psum2.tile([P, P], F32, name="y3_%d%d" % (mt, h), tag="y%d" % h)
                multiply(y3[mt, h][:], x_operand(D, o, h * P, (h + 1) * P), w_operand(D, o, mt * P, (mt + 1) * P), o)

        last_gated_pass(0)
        prepare(3, 1, [("v", 0, P), ("v", P, M)], halves)
        last_gated_pass(1)
        prepare(0, 0, [("v", 0, 160), ("s", 160, M)], halves)
        u3 = tile_at([P, HALVES, HALVES, P], F32, "u3", AT_RAW[0, 0])
        for mt, h in quarters:
            nc.scalar.activation(u3[:, mt, h, :], y3[mt, h][:], COPY, scale=gate_cols[:, D - 1, h : h + 1])
            turn(u3[:, mt, h, :], D, h, mt)

        y0 = {}
        for mt in range(HALVES):
            y0[mt, 0] = psum.tile([P, P], F32, name="y0_%d0" % mt, tag="self%d" % mt)
            y0[mt, 1] = psum2.tile([P, P], F32, name="y0_%d1" % mt, tag="y%d" % mt)

        def own_pass(o):
            for mt, h in quarters:
                multiply(y0[mt, h][:], w_operand(0, o, mt * P, (mt + 1) * P), x_operand(0, o, h * P, (h + 1) * P), o)

        own_pass(0)
        prepare(0, 1, [("v", 0, P), ("v", P, 192), ("s", 192, M)], halves)
        sums = tile_at([P, HALVES, V], F32, "sums", AT_RAW[0, 1])
        for mt in range(HALVES):
            nc.scalar.activation(sums[:, mt, :], gated[mt][:], COPY)
        own_pass(1)
        for mt in range(HALVES):
            res = keep.tile([P, V], F32, name="res%d" % mt)
            for h in range(HALVES):
                z = keep.tile([P, P], F32, name="z%d%d" % (mt, h))
                nc.vector.tensor_tensor(z[:], y0[mt, h][:], sums[:, mt, h * P : (h + 1) * P], ADD)
                nc.scalar.activation(res[:, h * P : (h + 1) * P], z[:], TANH)
            queue = nc.scalar if mt == HALVES - 1 else nc.sync
            queue.dma_start(out=out[mt * P : (mt + 1) * P, :], in_=res[:])
